import numpy as np
import ml_dtypes


def mxq(x, axis, fmt="e4m3"):
    dtype, down = {"e4m3": (ml_dtypes.float8_e4m3fn, 7), "e5m2": (ml_dtypes.float8_e5m2, 14)}[fmt]
    v = np.moveaxis(np.asarray(x, np.float32).astype(ml_dtypes.bfloat16).astype(np.float64), axis, -1)
    blocks = v.reshape(v.shape[:-1] + (-1, 32))
    amax = np.abs(blocks).max(-1, keepdims=True)
    byte = np.maximum(np.where(amax > 0, np.frexp(amax)[1] - 1 + 127, 0) - down, 1)
    scale = np.exp2(byte - 127.0)
    codes = (blocks / scale).astype(np.float32).astype(dtype).astype(np.float64)
    return np.moveaxis((codes * scale).reshape(v.shape), -1, axis)


WIDE = False


def mx_kscale(k):
    if not WIDE:
        return np.ones(k)
    levels = np.array([30, -30])
    if k % 512:
        return np.exp2(np.random.permutation(np.resize(levels, k // 32))).repeat(32)
    a = np.empty((k // 512, 16))
    for p in range(k // 512):
        a[p, :8] = np.random.permutation(np.resize(levels, 8))
        for g in range(8):
            far = levels[np.abs(levels - a[p, g]) >= 10]
            a[p, g + 8] = far[np.random.randint(len(far))]
    return np.exp2(a.ravel()).repeat(32)


def f64(x):
    return np.asarray(x).astype(np.float64)


def striped(idx):
    return np.tile(np.asarray(idx).reshape(-1, 16).T, (8, 1)).astype(np.uint16)


def unstriped(offs):
    return offs[:16].T.reshape(-1).astype(np.int64)


E2M1 = np.array([0.0, 0.5, 1.0, 1.5, 2.0, 3.0, 4.0, 6.0, -0.0, -0.5, -1.0, -1.5, -2.0, -3.0, -4.0, -6.0])


def pack_weight(w, fmt):
    k, n = w.shape
    w = f64(np.asarray(w, np.float32).astype(ml_dtypes.bfloat16)).reshape(k // 32, 32, n)
    amax = np.abs(w).max(1)
    if fmt == "e4m3":
        byte = np.frexp(amax)[1] - 1 + 127 - 7
    else:
        mant, ex = np.frexp(amax / 6.0)
        byte = np.where(mant > 0.5, ex, ex - 1) + 127
    byte = np.clip(np.where(amax > 0, byte, 1), 1, 254)
    scaled = (w * np.exp2(127.0 - byte)[:, None, :]).reshape(k, n).astype(np.float32)
    by_word = np.ascontiguousarray(scaled.reshape(k // 512, 128, 4, n).transpose(0, 1, 3, 2))
    if fmt == "e4m3":
        words = by_word.astype(ml_dtypes.float8_e4m3fn).view(np.uint8)
    else:
        c = by_word.astype(ml_dtypes.float4_e2m1fn).view(np.uint8) & 0xF
        words = (c[..., 0::2] | (c[..., 1::2] << 4)).reshape(k // 512, 128, 2 * n)
    return np.ascontiguousarray(words), np.ascontiguousarray(byte.astype(np.uint8).reshape(k // 512, 16, n))


def unpack_weight(words, scales, fmt):
    g, _, n = scales.shape
    words = np.ascontiguousarray(words).reshape(g, 128, n, -1)
    if fmt == "e4m3":
        vals = words.view(ml_dtypes.float8_e4m3fn).astype(np.float64)
    else:
        nib = np.empty((g, 128, n, 4), np.uint8)
        nib[..., 0::2] = words & 0xF
        nib[..., 1::2] = words >> 4
        vals = E2M1[nib]
    vals = vals * np.repeat(np.exp2(scales.astype(np.float64) - 127.0), 8, axis=1)[..., None]
    return vals.transpose(0, 1, 3, 2).reshape(g * 512, n)


K, T, Z, J, R, C, O, N, L, E = 512, 1024, 1024, 256, 512, 512, 256, 256, 512, 1024


def setup_inputs():
    n = np.random.standard_normal
    idx = np.random.permutation(T)[:J]
    idx2 = np.random.permutation(Z)[:J]
    idx3 = np.random.permutation(C)[:J]
    idx4 = np.random.permutation(C)[:J]
    idx5 = np.random.permutation(C)[:O]
    idx6 = np.random.permutation(E)[:O]
    fk = mx_kscale(K)
    fr = mx_kscale(R)
    fl = mx_kscale(L)
    xtp = pack_weight(n((K, T)) / fk[:, None], "e2m1")
    xop = pack_weight(n((K, Z)) / fk[:, None], "e4m3")
    wp = pack_weight(n((K, R)) * 1 / np.sqrt(K) * fk[:, None] * fr, "e4m3")
    wbp = pack_weight(n((R, N)) * 1 / np.sqrt(R) / fr[:, None], "e2m1")
    sxp = pack_weight(n((L, O)) / fl[:, None], "e4m3")
    wsp = pack_weight(n((L, N)) * 1 / np.sqrt(L) * fl[:, None], "e4m3")
    return {
        "xt_words": xtp[0],
        "xt_scales": xtp[1],
        "xo_words": xop[0],
        "xo_scales": xop[1],
        "w_words": wp[0],
        "w_scales": wp[1],
        "wb_words": wbp[0],
        "wb_scales": wbp[1],
        "sx_words": sxp[0],
        "sx_scales": sxp[1],
        "ws_words": wsp[0],
        "ws_scales": wsp[1],
        "offs": striped(idx),
        "offs2": striped(idx2),
        "offs3": striped(idx3),
        "offs4": striped(idx4),
        "offs5": striped(idx5),
        "offs6": striped(idx6),
    }


def reference(xt_words, xt_scales, xo_words, xo_scales, w_words, w_scales, wb_words, wb_scales, sx_words, sx_scales, ws_words, ws_scales, offs, offs2, offs3, offs4, offs5, offs6):
    idx = unstriped(offs)
    idx2 = unstriped(offs2)
    idx3 = unstriped(offs3)
    idx4 = unstriped(offs4)
    idx5 = unstriped(offs5)
    idx6 = unstriped(offs6)
    xtu = unpack_weight(xt_words, xt_scales, "e2m1")
    xou = unpack_weight(xo_words, xo_scales, "e4m3")
    wu = unpack_weight(w_words, w_scales, "e4m3")
    wbu = unpack_weight(wb_words, wb_scales, "e2m1")
    sxu = unpack_weight(sx_words, sx_scales, "e4m3")
    wsu = unpack_weight(ws_words, ws_scales, "e4m3")
    xtidxg = xtu[:, idx]
    a = wu.T @ xtidxg
    xoidx2g = xou[:, idx2]
    b = wu.T @ xoidx2g
    pw = np.zeros((R, C))
    pw[:, idx3] = a
    pv = np.zeros((R, C))
    pv[:, idx4] = b
    pg = pw + pv
    hid = pg[:, idx5]
    hidq = mxq(hid, 0, "e5m2")
    p = wbu.T @ hidq + wsu.T @ sxu
    y = np.zeros((N, E))
    y[:, idx6] = p
    return y

@@ -1,0 +1,178 @@
+from contextlib import ExitStack
+
+import concourse.mybir as mybir
+
+K, T, Z, J, R, C, O, N, L, E = 512, 1024, 1024, 256, 512, 512, 256, 256, 512, 1024
+FLOPS = 2 * (2 * K * R * J + R * N * O + L * N * O)
+
+F32 = mybir.dt.float32
+BF16 = mybir.dt.bfloat16
+I32 = mybir.dt.int32
+U32 = mybir.dt.uint32
+U16 = mybir.dt.uint16
+U8 = mybir.dt.uint8
+E4M3 = mybir.dt.float8_e4m3fn_x4
+E5M2 = mybir.dt.float8_e5m2_x4
+E2M1 = mybir.dt.float4_e2m1fn_x4
+COPY = mybir.ActivationFunctionType.Copy
+ADD = mybir.AluOpType.add
+
+P = 128
+PACK = 4
+
+
+def load_scale_rows(queues, plane, scales):
+    for q in range(4):
+        queues[q].dma_start(out=plane[32 * q : 32 * q + 4, :].bitcast(I32), in_=scales[0, 4 * q : 4 * q + 4, :].bitcast(I32))
+
+
+def words_view(words):
+    return words[0].rearrange("p n t -> p (n t)").bitcast(I32)
+
+
+def tile_list_oneforboth_shared_skip_scattered_kernel(
+    tc, xt_words, xt_scales, xo_words, xo_scales, w_words, w_scales, wb_words, wb_scales,
+    sx_words, sx_scales, ws_words, ws_scales, offs, offs2, offs3, offs4, offs5, offs6, out,
+):
+    nc = tc.nc
+    with ExitStack() as ctx:
+        lists = ctx.enter_context(tc.tile_pool(name="lists", bufs=1))
+        keep = ctx.enter_context(tc.tile_pool(name="keep", bufs=1))
+        psum = ctx.enter_context(tc.psum_pool(name="psum", bufs=1))
+
+        tok_list = lists.tile([P, J // 16], U16, name="tok_list")
+        note_list = lists.tile([P, J // 16], U16, name="note_list")
+        a_list = lists.tile([P, J // 16], U16, name="a_list")
+        b_list = lists.tile([P, J // 16], U16, name="b_list")
+        read_list = lists.tile([P, O // 16], U16, name="read_list")
+        page_list = lists.tile([P, O // 16], U16, name="page_list")
+
+        xt_w = keep.tile([P, T], U16, name="xt_w", tag="late0", align_bytes=64)
+        xo_w = keep.tile([P, Z], U32, name="xo_w", tag="slot1", align_bytes=64)
+        xt_s = keep.tile([P, T], U8, name="xt_s", tag="late2", align_bytes=64)
+        xo_s = keep.tile([P, Z], U8, name="xo_s", tag="slot6", align_bytes=64)
+        w_w = keep.tile([P, R], U32, name="w_w", tag="late1", align_bytes=64)
+        w_s = keep.tile([P, R], U8, name="w_s", tag="slot0", align_bytes=64)
+        late_s = keep.tile([P, 3 * N], U8, name="late_s", align_bytes=64)
+        wb_s, sx_s, ws_s = late_s[:, 0:N], late_s[:, N : 2 * N], late_s[:, 2 * N : 3 * N]
+
+        nc.vector.memset(xt_s[:].bitcast(I32), 0)
+        nc.vector.memset(w_s[:].bitcast(I32), 0)
+        nc.vector.memset(xo_s[:].bitcast(I32), 0)
+
+        sy, sc = nc.sync, nc.scalar
+        sc.dma_start(out=xt_w[:].bitcast(I32), in_=xt_words[0].bitcast(I32))
+        sy.dma_start(tok_list[:], offs)
+        sc.dma_start(out=w_w[:].bitcast(I32), in_=words_view(w_words))
+        load_scale_rows((sy, sc, sy, sc), xt_s, xt_scales)
+        load_scale_rows((sy, sc, sy, sc), w_s, w_scales)
+        sy.dma_start(note_list[:], offs2)
+        sy.dma_start(out=xo_w[:].bitcast(I32), in_=words_view(xo_words))
+        load_scale_rows((sy, nc.gpsimd, sy, nc.gpsimd), xo_s, xo_scales)
+        sy.dma_start(a_list[:], offs3)
+        sy.dma_start(b_list[:], offs4)
+        sy.dma_start(read_list[:], offs5)
+        sy.dma_start(page_list[:], offs6)
+
+        xt_gw = keep.tile([P, J], U16, name="xt_gw", align_bytes=64)
+        xt_gs = keep.tile([P, J], U8, name="xt_gs", align_bytes=64)
+        xo_gw = keep.tile([P, J], U32, name="xo_gw", align_bytes=64)
+        xo_gs = keep.tile([P, J], U8, name="xo_gs", align_bytes=64)
+        wd_w = keep.tile([P, PACK, P], U32, name="wd_w", tag="slot4", align_bytes=64)
+        wd_s = keep.tile([P, PACK, P], U8, name="wd_s", tag="slot3", align_bytes=64)
+
+        nc.vector.tensor_copy(xt_gw[:], xt_w[:].indirect(tok_list[:]))
+        nc.vector.tensor_copy(xt_gs[:], xt_s[:].indirect(tok_list[:]))
+        nc.vector.tensor_copy(wd_w[:], w_w[:].rearrange("p (m t) -> p t m", t=PACK))
+        nc.vector.tensor_copy(wd_s[:], w_s[:].rearrange("p (m t) -> p t m", t=PACK))
+        nc.vector.tensor_copy(xo_gw[:], xo_w[:].indirect(note_list[:]))
+        nc.vector.tensor_copy(xo_gs[:], xo_s[:].indirect(note_list[:]))
+
+        pw = [keep.tile([P, C], F32, name=f"pw{t}") for t in range(PACK)]
+        for t in range(PACK):
+            nc.vector.memset(pw[t][:], 0.0)
+        nc.vector.memset(late_s[:].bitcast(I32), 0)
+        sx_w = keep.tile([P, O], U32, name="sx_w", tag="late0", align_bytes=64)
+        ws_w = keep.tile([P, N], U32, name="ws_w", tag="late1", align_bytes=64)
+        wb_w = keep.tile([P, 2 * N], U8, name="wb_w", tag="late2", align_bytes=64)
+        sy.dma_start(out=sx_w[:].bitcast(I32), in_=words_view(sx_words))
+        sy.dma_start(out=ws_w[:].bitcast(I32), in_=words_view(ws_words))
+        sy.dma_start(out=wb_w[:].bitcast(I32), in_=wb_words[0].bitcast(I32))
+        load_scale_rows((sy, sy, sy, sy), sx_s, sx_scales)
+        load_scale_rows((sy, sy, sy, sy), ws_s, ws_scales)
+        load_scale_rows((sy, sy, sy, sy), wb_s, wb_scales)
+
+        a_ps = [psum.tile([P, J], F32, name=f"a_ps{t}") for t in range(PACK)]
+        b_ps = [psum.tile([P, 2, J], F32, name=f"b_ps{u}") for u in range(2)]
+        p_ps = [psum.tile([P, O], F32, name=f"p_ps{h}") for h in range(2)]
+        a_sb = [keep.tile([P, J], F32, name=f"a_sb{t}", tag=("slot2", "slot6", "slot5", "slot7")[t], align_bytes=64) for t in range(PACK)]
+        b_sb = [keep.tile([P, 2, J], F32, name=f"b_sb{u}") for u in range(2)]
+        for t in range(PACK):
+            nc.tensor.matmul_mx(
+                out=a_ps[t][:], lhsT=wd_w[:, t, :].bitcast(E4M3), lhsT_scale=wd_s[:, t, :],
+                rhs=xt_gw[:].bitcast(E2M1), rhs_scale=xt_gs[:], start=True, stop=True,
+            )
+        for t in range(PACK):
+            nc.tensor.matmul_mx(
+                out=b_ps[t // 2][:, t % 2, :], lhsT=wd_w[:, t, :].bitcast(E4M3), lhsT_scale=wd_s[:, t, :],
+                rhs=xo_gw[:].bitcast(E4M3), rhs_scale=xo_gs[:], start=True, stop=True,
+            )
+        for h in range(2):
+            nc.tensor.matmul_mx(
+                out=p_ps[h][:], lhsT=ws_w[:, h * P : (h + 1) * P].bitcast(E4M3), lhsT_scale=ws_s[:, h * P : (h + 1) * P],
+                rhs=sx_w[:].bitcast(E4M3), rhs_scale=sx_s, start=True, stop=False,
+            )
+
+        pg = [keep.tile([P, C], F32, name=f"pg{t}") for t in range(PACK)]
+        hid = keep.tile([P, O, PACK], BF16, name="hid", align_bytes=64)
+        rows = keep.tile([P, PACK - 1, O], BF16, name="rows", align_bytes=64)
+
+        def scatter_s(window, offsets, values):
+            nc.scalar.activation(window[:].indirect(offsets[:]), values, COPY)
+
+        def scatter_v(window, offsets, values):
+            nc.vector.tensor_copy(window[:].indirect(offsets[:]), values)
+
+        nc.scalar.copy(a_sb[0][:], a_ps[0][:])
+        scatter_s(pw[0], a_list, a_sb[0][:])
+        nc.vector.tensor_copy(a_sb[1][:], a_ps[1][:])
+        scatter_v(pw[1], a_list, a_sb[1][:])
+        nc.scalar.copy(a_sb[3][:], a_ps[3][:])
+        nc.scalar.copy(a_sb[2][:], a_ps[2][:])
+        scatter_s(pw[2], a_list, a_sb[2][:])
+        scatter_v(pw[3], a_list, a_sb[3][:])
+        pv = [keep.tile([P, C], F32, name=f"pv{t}", tag=f"slot{t}", align_bytes=64) for t in range(PACK)]
+        for t in range(PACK):
+            nc.gpsimd.memset(pv[t][:], 0.0)
+        nc.scalar.copy(b_sb[0][:], b_ps[0][:])
+        nc.scalar.copy(b_sb[1][:], b_ps[1][:])
+        scatter_v(pv[0], b_list, b_sb[0][:, 0, :])
+        scatter_s(pv[1], b_list, b_sb[0][:, 1, :])
+        nc.vector.tensor_tensor(pg[0][:], pw[0][:], pv[0][:], ADD)
+        scatter_v(pv[2], b_list, b_sb[1][:, 0, :])
+        scatter_s(pv[3], b_list, b_sb[1][:, 1, :])
+        for t in range(1, PACK):
+            nc.vector.tensor_tensor(pg[t][:], pw[t][:], pv[t][:], ADD)
+        for t in range(PACK - 1):
+            nc.scalar.activation(rows[:, t, :], pg[t][:].indirect(read_list[:]), COPY)
+        nc.vector.tensor_copy(hid[:, :, PACK - 1], pg[PACK - 1][:].indirect(read_list[:]))
+        nc.vector.tensor_copy(hid[:, :, 0 : PACK - 1], rows[:].rearrange("p t o -> p o t"))
+
+        page = [keep.tile([P, E], F32, name=f"page{h}", tag=f"slot{4 + h}", align_bytes=64) for h in range(2)]
+        for h in range(2):
+            nc.gpsimd.memset(page[h][:], 0.0)
+        hid_w = keep.tile([P, O], U32, name="hid_w", align_bytes=64)
+        hid_s = keep.tile([P, O], U8, name="hid_s", align_bytes=64)
+        nc.vector.quantize_mx(out=hid_w[:].bitcast(E5M2), scales=hid_s[:], in_=hid[:].rearrange("p o t -> p (o t)"))
+        p_sb = [keep.tile([P, O], F32, name=f"p_sb{h}") for h in range(2)]
+        for h in range(2):
+            nc.tensor.matmul_mx(
+                out=p_ps[h][:], lhsT=wb_w[:, 2 * h * P : 2 * (h + 1) * P].bitcast(E2M1), lhsT_scale=wb_s[:, h * P : (h + 1) * P],
+                rhs=hid_w[:].bitcast(E5M2), rhs_scale=hid_s[:], start=False, stop=True,
+            )
+        nc.scalar.copy(p_sb[0][:], p_ps[0][:])
+        nc.scalar.activation(page[0][:].indirect(page_list[:]), p_sb[0][:], COPY)
+        nc.vector.tensor_copy(p_sb[1][:], p_ps[1][:])
+        nc.vector.tensor_copy(page[1][:].indirect(page_list[:]), p_sb[1][:])
+        for h in range(2):
+            nc.sync.dma_start(out=out[h * P : (h + 1) * P, :], in_=page[h][:])

@@ -38,6 +38,7 @@ def tile_list_oneforboth_shared_skip_scattered_kernel(
     with ExitStack() as ctx:
         lists = ctx.enter_context(tc.tile_pool(name="lists", bufs=1))
         keep = ctx.enter_context(tc.tile_pool(name="keep", bufs=1))
+        tail = ctx.enter_context(tc.tile_pool(name="tail", bufs=1))
         psum = ctx.enter_context(tc.psum_pool(name="psum", bufs=1))
 
         tok_list = lists.tile([P, J // 16], U16, name="tok_list")
@@ -48,27 +49,32 @@ def tile_list_oneforboth_shared_skip_scattered_kernel(
         page_list = lists.tile([P, O // 16], U16, name="page_list")
 
         xt_w = keep.tile([P, T], U16, name="xt_w", tag="late0", align_bytes=64)
-        xo_w = keep.tile([P, Z], U32, name="xo_w", tag="slot1", align_bytes=64)
+        xo_w = keep.tile([P, Z], U32, name="xo_w", align_bytes=64)
         xt_s = keep.tile([P, T], U8, name="xt_s", tag="late2", align_bytes=64)
-        xo_s = keep.tile([P, Z], U8, name="xo_s", tag="slot6", align_bytes=64)
+        xo_s = keep.tile([P, Z], U8, name="xo_s", align_bytes=64)
         w_w = keep.tile([P, R], U32, name="w_w", tag="late1", align_bytes=64)
-        w_s = keep.tile([P, R], U8, name="w_s", tag="slot0", align_bytes=64)
+        w_s = keep.tile([P, R], U8, name="w_s", align_bytes=64)
         late_s = keep.tile([P, 3 * N], U8, name="late_s", align_bytes=64)
         wb_s, sx_s, ws_s = late_s[:, 0:N], late_s[:, N : 2 * N], late_s[:, 2 * N : 3 * N]
 
         nc.vector.memset(xt_s[:].bitcast(I32), 0)
         nc.vector.memset(w_s[:].bitcast(I32), 0)
         nc.vector.memset(xo_s[:].bitcast(I32), 0)
+        pw = [keep.tile([P, C], F32, name=f"pw{t}") for t in range(PACK)]
+        pv = [keep.tile([P, C], F32, name=f"pv{t}") for t in range(PACK)]
+        for board in pw + pv:
+            nc.vector.memset(board[:].bitcast(I32), 0)
+        nc.vector.memset(late_s[:].bitcast(I32), 0)
 
         sy, sc = nc.sync, nc.scalar
         sc.dma_start(out=xt_w[:].bitcast(I32), in_=xt_words[0].bitcast(I32))
         sy.dma_start(tok_list[:], offs)
         sc.dma_start(out=w_w[:].bitcast(I32), in_=words_view(w_words))
         load_scale_rows((sy, sc, sy, sc), xt_s, xt_scales)
-        load_scale_rows((sy, sc, sy, sc), w_s, w_scales)
+        load_scale_rows((sy, sy, sy, sy), w_s, w_scales)
         sy.dma_start(note_list[:], offs2)
         sy.dma_start(out=xo_w[:].bitcast(I32), in_=words_view(xo_words))
-        load_scale_rows((sy, nc.gpsimd, sy, nc.gpsimd), xo_s, xo_scales)
+        load_scale_rows((sy, sy, sy, sy), xo_s, xo_scales)
         sy.dma_start(a_list[:], offs3)
         sy.dma_start(b_list[:], offs4)
         sy.dma_start(read_list[:], offs5)
@@ -78,20 +84,20 @@ def tile_list_oneforboth_shared_skip_scattered_kernel(
         xt_gs = keep.tile([P, J], U8, name="xt_gs", align_bytes=64)
         xo_gw = keep.tile([P, J], U32, name="xo_gw", align_bytes=64)
         xo_gs = keep.tile([P, J], U8, name="xo_gs", align_bytes=64)
-        wd_w = keep.tile([P, PACK, P], U32, name="wd_w", tag="slot4", align_bytes=64)
-        wd_s = keep.tile([P, PACK, P], U8, name="wd_s", tag="slot3", align_bytes=64)
+        wd_w = keep.tile([P, PACK, P], U32, name="wd_w", align_bytes=64)
+        wd_s = keep.tile([P, PACK, P], U8, name="wd_s", align_bytes=64)
 
         nc.vector.tensor_copy(xt_gw[:], xt_w[:].indirect(tok_list[:]))
         nc.vector.tensor_copy(xt_gs[:], xt_s[:].indirect(tok_list[:]))
-        nc.vector.tensor_copy(wd_w[:], w_w[:].rearrange("p (m t) -> p t m", t=PACK))
-        nc.vector.tensor_copy(wd_s[:], w_s[:].rearrange("p (m t) -> p t m", t=PACK))
+        nc.vector.tensor_copy(
+            wd_w[:].rearrange("p t (c i) -> p c t i", i=4), w_w[:].rearrange("p (c i t) -> p c t i", i=4, t=PACK)
+        )
+        nc.vector.tensor_copy(
+            wd_s[:].rearrange("p t (c i) -> p c t i", i=16), w_s[:].rearrange("p (c i t) -> p c t i", i=16, t=PACK)
+        )
         nc.vector.tensor_copy(xo_gw[:], xo_w[:].indirect(note_list[:]))
         nc.vector.tensor_copy(xo_gs[:], xo_s[:].indirect(note_list[:]))
 
-        pw = [keep.tile([P, C], F32, name=f"pw{t}") for t in range(PACK)]
-        for t in range(PACK):
-            nc.vector.memset(pw[t][:], 0.0)
-        nc.vector.memset(late_s[:].bitcast(I32), 0)
         sx_w = keep.tile([P, O], U32, name="sx_w", tag="late0", align_bytes=64)
         ws_w = keep.tile([P, N], U32, name="ws_w", tag="late1", align_bytes=64)
         wb_w = keep.tile([P, 2 * N], U8, name="wb_w", tag="late2", align_bytes=64)
@@ -102,30 +108,11 @@ def tile_list_oneforboth_shared_skip_scattered_kernel(
         load_scale_rows((sy, sy, sy, sy), ws_s, ws_scales)
         load_scale_rows((sy, sy, sy, sy), wb_s, wb_scales)
 
-        a_ps = [psum.tile([P, J], F32, name=f"a_ps{t}") for t in range(PACK)]
-        b_ps = [psum.tile([P, 2, J], F32, name=f"b_ps{u}") for u in range(2)]
-        p_ps = [psum.tile([P, O], F32, name=f"p_ps{h}") for h in range(2)]
-        a_sb = [keep.tile([P, J], F32, name=f"a_sb{t}", tag=("slot2", "slot6", "slot5", "slot7")[t], align_bytes=64) for t in range(PACK)]
-        b_sb = [keep.tile([P, 2, J], F32, name=f"b_sb{u}") for u in range(2)]
-        for t in range(PACK):
+        def first_stage(bank, t, words, scales):
             nc.tensor.matmul_mx(
-                out=a_ps[t][:], lhsT=wd_w[:, t, :].bitcast(E4M3), lhsT_scale=wd_s[:, t, :],
-                rhs=xt_gw[:].bitcast(E2M1), rhs_scale=xt_gs[:], start=True, stop=True,
+                out=bank, lhsT=wd_w[:, t, :].bitcast(E4M3), lhsT_scale=wd_s[:, t, :],
+                rhs=words, rhs_scale=scales, start=True, stop=True,
             )
-        for t in range(PACK):
-            nc.tensor.matmul_mx(
-                out=b_ps[t // 2][:, t % 2, :], lhsT=wd_w[:, t, :].bitcast(E4M3), lhsT_scale=wd_s[:, t, :],
-                rhs=xo_gw[:].bitcast(E4M3), rhs_scale=xo_gs[:], start=True, stop=True,
-            )
-        for h in range(2):
-            nc.tensor.matmul_mx(
-                out=p_ps[h][:], lhsT=ws_w[:, h * P : (h + 1) * P].bitcast(E4M3), lhsT_scale=ws_s[:, h * P : (h + 1) * P],
-                rhs=sx_w[:].bitcast(E4M3), rhs_scale=sx_s, start=True, stop=False,
-            )
-
-        pg = [keep.tile([P, C], F32, name=f"pg{t}") for t in range(PACK)]
-        hid = keep.tile([P, O, PACK], BF16, name="hid", align_bytes=64)
-        rows = keep.tile([P, PACK - 1, O], BF16, name="rows", align_bytes=64)
 
         def scatter_s(window, offsets, values):
             nc.scalar.activation(window[:].indirect(offsets[:]), values, COPY)
@@ -133,37 +120,52 @@ def tile_list_oneforboth_shared_skip_scattered_kernel(
         def scatter_v(window, offsets, values):
             nc.vector.tensor_copy(window[:].indirect(offsets[:]), values)
 
-        nc.scalar.copy(a_sb[0][:], a_ps[0][:])
+        a_sb = [keep.tile([P, J], F32, name=f"a_sb{t}") for t in range(PACK)]
+        b_sb = [keep.tile([P, 2, J], F32, name=f"b_sb{u}") for u in range(2)]
+        for t in (0, 1, 3):
+            a_ps = psum.tile([P, J], F32, name=f"a_ps{t}")
+            first_stage(a_ps[:], t, xt_gw[:].bitcast(E2M1), xt_gs[:])
+            nc.scalar.copy(a_sb[t][:], a_ps[:])
         scatter_s(pw[0], a_list, a_sb[0][:])
-        nc.vector.tensor_copy(a_sb[1][:], a_ps[1][:])
         scatter_v(pw[1], a_list, a_sb[1][:])
-        nc.scalar.copy(a_sb[3][:], a_ps[3][:])
-        nc.scalar.copy(a_sb[2][:], a_ps[2][:])
-        scatter_s(pw[2], a_list, a_sb[2][:])
         scatter_v(pw[3], a_list, a_sb[3][:])
-        pv = [keep.tile([P, C], F32, name=f"pv{t}", tag=f"slot{t}", align_bytes=64) for t in range(PACK)]
-        for t in range(PACK):
-            nc.gpsimd.memset(pv[t][:], 0.0)
-        nc.scalar.copy(b_sb[0][:], b_ps[0][:])
-        nc.scalar.copy(b_sb[1][:], b_ps[1][:])
+        for u in range(2):
+            b_ps = psum.tile([P, 2, J], F32, name=f"b_ps{u}")
+            for v in range(2):
+                first_stage(b_ps[:, v, :], 2 * u + v, xo_gw[:].bitcast(E4M3), xo_gs[:])
+            nc.scalar.copy(b_sb[u][:], b_ps[:])
+        a_ps = psum.tile([P, J], F32, name="a_ps2", tag="b_ps0")
+        first_stage(a_ps[:], 2, xt_gw[:].bitcast(E2M1), xt_gs[:])
+        nc.scalar.copy(a_sb[2][:], a_ps[:])
+        p_ps = [psum.tile([P, O], F32, name=f"p_ps{h}", tag=("b_ps1", "b_ps0")[h]) for h in range(2)]
+        for h in range(2):
+            nc.tensor.matmul_mx(
+                out=p_ps[h][:], lhsT=ws_w[:, h * P : (h + 1) * P].bitcast(E4M3), lhsT_scale=ws_s[:, h * P : (h + 1) * P],
+                rhs=sx_w[:].bitcast(E4M3), rhs_scale=sx_s, start=True, stop=False,
+            )
         scatter_v(pv[0], b_list, b_sb[0][:, 0, :])
         scatter_s(pv[1], b_list, b_sb[0][:, 1, :])
-        nc.vector.tensor_tensor(pg[0][:], pw[0][:], pv[0][:], ADD)
+        scatter_s(pw[2], a_list, a_sb[2][:])
         scatter_v(pv[2], b_list, b_sb[1][:, 0, :])
         scatter_s(pv[3], b_list, b_sb[1][:, 1, :])
-        for t in range(1, PACK):
-            nc.vector.tensor_tensor(pg[t][:], pw[t][:], pv[t][:], ADD)
-        for t in range(PACK - 1):
-            nc.scalar.activation(rows[:, t, :], pg[t][:].indirect(read_list[:]), COPY)
-        nc.vector.tensor_copy(hid[:, :, PACK - 1], pg[PACK - 1][:].indirect(read_list[:]))
-        nc.vector.tensor_copy(hid[:, :, 0 : PACK - 1], rows[:].rearrange("p t o -> p o t"))
 
-        page = [keep.tile([P, E], F32, name=f"page{h}", tag=f"slot{4 + h}", align_bytes=64) for h in range(2)]
-        for h in range(2):
-            nc.gpsimd.memset(page[h][:], 0.0)
+        pg = [keep.tile([P, C], F32, name=f"pg{t}") for t in range(PACK)]
+        hid = tail.tile([P, O, PACK], BF16, name="hid", align_bytes=64, offset=3072)
+        rows = keep.tile([P, PACK, O], BF16, name="rows", align_bytes=64)
+        for t in range(PACK):
+            nc.vector.tensor_tensor(pg[t][:], pw[t][:], pv[t][:], ADD)
+        for t in range(2):
+            nc.scalar.activation(rows[:, t, :], pg[t][:].indirect(read_list[:]), COPY)
+        for t in range(2, PACK):
+            nc.vector.tensor_copy(rows[:, t, :], pg[t][:].indirect(read_list[:]))
+        nc.vector.tensor_copy(hid[:].rearrange("p (c i) t -> p c t i", i=4), rows[:].rearrange("p t (c i) -> p c t i", i=4))
+
         hid_w = keep.tile([P, O], U32, name="hid_w", align_bytes=64)
         hid_s = keep.tile([P, O], U8, name="hid_s", align_bytes=64)
         nc.vector.quantize_mx(out=hid_w[:].bitcast(E5M2), scales=hid_s[:], in_=hid[:].rearrange("p o t -> p (o t)"))
+        page = [tail.tile([P, E], F32, name=f"page{h}", align_bytes=64, offset=4096 * h) for h in range(2)]
+        for h in range(2):
+            nc.vector.memset(page[h][:].bitcast(I32), 0)
         p_sb = [keep.tile([P, O], F32, name=f"p_sb{h}") for h in range(2)]
         for h in range(2):
             nc.tensor.matmul_mx(

@@ -137,11 +137,18 @@ def tile_list_oneforboth_shared_skip_scattered_kernel(
         a_ps = psum.tile([P, J], F32, name="a_ps2", tag="b_ps0")
         first_stage(a_ps[:], 2, xt_gw[:].bitcast(E2M1), xt_gs[:])
         nc.scalar.copy(a_sb[2][:], a_ps[:])
-        p_ps = [psum.tile([P, O], F32, name=f"p_ps{h}", tag=("b_ps1", "b_ps0")[h]) for h in range(2)]
-        for h in range(2):
+        half = O // 2
+        halves = [slice(0, half), slice(half, O)]
+        list_halves = [slice(0, half // 16), slice(half // 16, O // 16)]
+        sums = [
+            (0, halves[0], psum.tile([P, half], F32, name="p0_lo", tag="b_ps1")),
+            (0, halves[1], psum.tile([P, half], F32, name="p0_hi", tag="a_ps3")),
+            (1, slice(0, O), psum.tile([P, O], F32, name="p1", tag="b_ps0")),
+        ]
+        for h, cols, bank in sums:
             nc.tensor.matmul_mx(
-                out=p_ps[h][:], lhsT=ws_w[:, h * P : (h + 1) * P].bitcast(E4M3), lhsT_scale=ws_s[:, h * P : (h + 1) * P],
-                rhs=sx_w[:].bitcast(E4M3), rhs_scale=sx_s, start=True, stop=False,
+                out=bank[:], lhsT=ws_w[:, h * P : (h + 1) * P].bitcast(E4M3), lhsT_scale=ws_s[:, h * P : (h + 1) * P],
+                rhs=sx_w[:, cols].bitcast(E4M3), rhs_scale=sx_s[:, cols], start=True, stop=False,
             )
         scatter_v(pv[0], b_list, b_sb[0][:, 0, :])
         scatter_s(pv[1], b_list, b_sb[0][:, 1, :])
@@ -150,31 +157,52 @@ def tile_list_oneforboth_shared_skip_scattered_kernel(
         scatter_s(pv[3], b_list, b_sb[1][:, 1, :])
 
         pg = [keep.tile([P, C], F32, name=f"pg{t}") for t in range(PACK)]
-        hid = tail.tile([P, O, PACK], BF16, name="hid", align_bytes=64, offset=3072)
-        rows = keep.tile([P, PACK, O], BF16, name="rows", align_bytes=64)
-        for t in range(PACK):
-            nc.vector.tensor_tensor(pg[t][:], pw[t][:], pv[t][:], ADD)
-        for t in range(2):
-            nc.scalar.activation(rows[:, t, :], pg[t][:].indirect(read_list[:]), COPY)
-        for t in range(2, PACK):
-            nc.vector.tensor_copy(rows[:, t, :], pg[t][:].indirect(read_list[:]))
-        nc.vector.tensor_copy(hid[:].rearrange("p (c i) t -> p c t i", i=4), rows[:].rearrange("p t (c i) -> p c t i", i=4))
-
+        hid = [tail.tile([P, half, PACK], BF16, name=f"hid{u}", align_bytes=64, offset=3072 + 1024 * u) for u in range(2)]
+        rows = [keep.tile([P, PACK, half], BF16, name=f"rows{u}", align_bytes=64) for u in range(2)]
         hid_w = keep.tile([P, O], U32, name="hid_w", align_bytes=64)
         hid_s = keep.tile([P, O], U8, name="hid_s", align_bytes=64)
-        nc.vector.quantize_mx(out=hid_w[:].bitcast(E5M2), scales=hid_s[:], in_=hid[:].rearrange("p o t -> p (o t)"))
-        page = [tail.tile([P, E], F32, name=f"page{h}", align_bytes=64, offset=4096 * h) for h in range(2)]
-        for h in range(2):
-            nc.vector.memset(page[h][:].bitcast(I32), 0)
-        p_sb = [keep.tile([P, O], F32, name=f"p_sb{h}") for h in range(2)]
-        for h in range(2):
-            nc.tensor.matmul_mx(
-                out=p_ps[h][:], lhsT=wb_w[:, 2 * h * P : 2 * (h + 1) * P].bitcast(E2M1), lhsT_scale=wb_s[:, h * P : (h + 1) * P],
-                rhs=hid_w[:].bitcast(E5M2), rhs_scale=hid_s[:], start=False, stop=True,
+
+        def read_s(t, u):
+            nc.scalar.activation(rows[u][:, t, :], pg[t][:].indirect(read_list[:, list_halves[u]]), COPY)
+
+        def read_v(t, u):
+            nc.vector.tensor_copy(rows[u][:, t, :], pg[t][:].indirect(read_list[:, list_halves[u]]))
+
+        def interleave(u):
+            nc.vector.tensor_copy(hid[u][:].rearrange("p (c i) t -> p c t i", i=4), rows[u][:].rearrange("p t (c i) -> p c t i", i=4))
+
+        def quantise(u):
+            nc.vector.quantize_mx(
+                out=hid_w[:, halves[u]].bitcast(E5M2), scales=hid_s[:, halves[u]], in_=hid[u][:].rearrange("p o t -> p (o t)")
             )
-        nc.scalar.copy(p_sb[0][:], p_ps[0][:])
-        nc.scalar.activation(page[0][:].indirect(page_list[:]), p_sb[0][:], COPY)
-        nc.vector.tensor_copy(p_sb[1][:], p_ps[1][:])
+
+        def second_stage(h, cols, bank):
+            nc.tensor.matmul_mx(
+                out=bank[:], lhsT=wb_w[:, 2 * h * P : 2 * (h + 1) * P].bitcast(E2M1), lhsT_scale=wb_s[:, h * P : (h + 1) * P],
+                rhs=hid_w[:, cols].bitcast(E5M2), rhs_scale=hid_s[:, cols], start=False, stop=True,
+            )
+
+        for t in range(PACK):
+            nc.vector.tensor_tensor(pg[t][:], pw[t][:], pv[t][:], ADD)
+        for t, u in ((0, 0), (1, 0), (3, 0), (0, 1), (3, 1)):
+            read_s(t, u)
+        read_v(2, 0)
+        read_v(2, 1)
+        interleave(0)
+        read_v(1, 1)
+        quantise(0)
+        interleave(1)
+        page = [tail.tile([P, E], F32, name=f"page{h}", align_bytes=64, offset=4096 * h) for h in range(2)]
+        nc.vector.memset(page[0][:].bitcast(I32), 0)
+        quantise(1)
+        nc.vector.memset(page[1][:].bitcast(I32), 0)
+        p_sb = [keep.tile([P, O], F32, name=f"p_sb{h}") for h in range(2)]
+        for h, cols, bank in sums:
+            second_stage(h, cols, bank)
+        for u in range(2):
+            nc.scalar.copy(p_sb[0][:, halves[u]], sums[u][2][:])
+            nc.scalar.activation(page[0][:].indirect(page_list[:, list_halves[u]]), p_sb[0][:, halves[u]], COPY)
+        nc.vector.tensor_copy(p_sb[1][:], sums[2][2][:])
         nc.vector.tensor_copy(page[1][:].indirect(page_list[:]), p_sb[1][:])
         for h in range(2):
             nc.sync.dma_start(out=out[h * P : (h + 1) * P, :], in_=page[h][:])

@@ -19,11 +19,16 @@ ADD = mybir.AluOpType.add
 
 P = 128
 PACK = 4
+GROUP = 16
+HALF = O // 2
+LINE = 16
+PAGE_BYTES = 4 * E
+HID_BYTES = 2 * PACK * HALF
 
 
-def load_scale_rows(queues, plane, scales):
+def load_scale_rows(queue, tile, scales):
     for q in range(4):
-        queues[q].dma_start(out=plane[32 * q : 32 * q + 4, :].bitcast(I32), in_=scales[0, 4 * q : 4 * q + 4, :].bitcast(I32))
+        queue.dma_start(out=tile[32 * q : 32 * q + 4, :].bitcast(I32), in_=scales[0, 4 * q : 4 * q + 4, :].bitcast(I32))
 
 
 def words_view(words):
@@ -41,12 +46,12 @@ def tile_list_oneforboth_shared_skip_scattered_kernel(
         tail = ctx.enter_context(tc.tile_pool(name="tail", bufs=1))
         psum = ctx.enter_context(tc.psum_pool(name="psum", bufs=1))
 
-        tok_list = lists.tile([P, J // 16], U16, name="tok_list")
-        note_list = lists.tile([P, J // 16], U16, name="note_list")
-        a_list = lists.tile([P, J // 16], U16, name="a_list")
-        b_list = lists.tile([P, J // 16], U16, name="b_list")
-        read_list = lists.tile([P, O // 16], U16, name="read_list")
-        page_list = lists.tile([P, O // 16], U16, name="page_list")
+        tok_list = lists.tile([P, J // GROUP], U16, name="tok_list")
+        note_list = lists.tile([P, J // GROUP], U16, name="note_list")
+        a_list = lists.tile([P, J // GROUP], U16, name="a_list")
+        b_list = lists.tile([P, J // GROUP], U16, name="b_list")
+        read_list = lists.tile([P, O // GROUP], U16, name="read_list")
+        page_list = lists.tile([P, O // GROUP], U16, name="page_list")
 
         xt_w = keep.tile([P, T], U16, name="xt_w", tag="late0", align_bytes=64)
         xo_w = keep.tile([P, Z], U32, name="xo_w", align_bytes=64)
@@ -66,19 +71,18 @@ def tile_list_oneforboth_shared_skip_scattered_kernel(
             nc.vector.memset(board[:].bitcast(I32), 0)
         nc.vector.memset(late_s[:].bitcast(I32), 0)
 
-        sy, sc = nc.sync, nc.scalar
-        sc.dma_start(out=xt_w[:].bitcast(I32), in_=xt_words[0].bitcast(I32))
-        sy.dma_start(tok_list[:], offs)
-        sc.dma_start(out=w_w[:].bitcast(I32), in_=words_view(w_words))
-        load_scale_rows((sy, sc, sy, sc), xt_s, xt_scales)
-        load_scale_rows((sy, sy, sy, sy), w_s, w_scales)
-        sy.dma_start(note_list[:], offs2)
-        sy.dma_start(out=xo_w[:].bitcast(I32), in_=words_view(xo_words))
-        load_scale_rows((sy, sy, sy, sy), xo_s, xo_scales)
-        sy.dma_start(a_list[:], offs3)
-        sy.dma_start(b_list[:], offs4)
-        sy.dma_start(read_list[:], offs5)
-        sy.dma_start(page_list[:], offs6)
+        nc.sync.dma_start(tok_list[:], offs)
+        nc.sync.dma_start(out=xt_w[:].bitcast(I32), in_=xt_words[0].bitcast(I32))
+        nc.sync.dma_start(out=w_w[:].bitcast(I32), in_=words_view(w_words))
+        load_scale_rows(nc.scalar, xt_s, xt_scales)
+        nc.sync.dma_start(out=xo_w[:].bitcast(I32), in_=words_view(xo_words))
+        load_scale_rows(nc.sync, w_s, w_scales)
+        nc.sync.dma_start(note_list[:], offs2)
+        load_scale_rows(nc.sync, xo_s, xo_scales)
+        nc.sync.dma_start(a_list[:], offs3)
+        nc.sync.dma_start(b_list[:], offs4)
+        nc.sync.dma_start(read_list[:], offs5)
+        nc.sync.dma_start(page_list[:], offs6)
 
         xt_gw = keep.tile([P, J], U16, name="xt_gw", align_bytes=64)
         xt_gs = keep.tile([P, J], U8, name="xt_gs", align_bytes=64)
@@ -90,10 +94,12 @@ def tile_list_oneforboth_shared_skip_scattered_kernel(
         nc.vector.tensor_copy(xt_gw[:], xt_w[:].indirect(tok_list[:]))
         nc.vector.tensor_copy(xt_gs[:], xt_s[:].indirect(tok_list[:]))
         nc.vector.tensor_copy(
-            wd_w[:].rearrange("p t (c i) -> p c t i", i=4), w_w[:].rearrange("p (c i t) -> p c t i", i=4, t=PACK)
+            wd_w[:].rearrange("p t (c i) -> p c t i", i=LINE // 4),
+            w_w[:].rearrange("p (c i t) -> p c t i", i=LINE // 4, t=PACK),
         )
         nc.vector.tensor_copy(
-            wd_s[:].rearrange("p t (c i) -> p c t i", i=16), w_s[:].rearrange("p (c i t) -> p c t i", i=16, t=PACK)
+            wd_s[:].rearrange("p t (c i) -> p c t i", i=LINE),
+            w_s[:].rearrange("p (c i t) -> p c t i", i=LINE, t=PACK),
         )
         nc.vector.tensor_copy(xo_gw[:], xo_w[:].indirect(note_list[:]))
         nc.vector.tensor_copy(xo_gs[:], xo_s[:].indirect(note_list[:]))
@@ -101,12 +107,12 @@ def tile_list_oneforboth_shared_skip_scattered_kernel(
         sx_w = keep.tile([P, O], U32, name="sx_w", tag="late0", align_bytes=64)
         ws_w = keep.tile([P, N], U32, name="ws_w", tag="late1", align_bytes=64)
         wb_w = keep.tile([P, 2 * N], U8, name="wb_w", tag="late2", align_bytes=64)
-        sy.dma_start(out=sx_w[:].bitcast(I32), in_=words_view(sx_words))
-        sy.dma_start(out=ws_w[:].bitcast(I32), in_=words_view(ws_words))
-        sy.dma_start(out=wb_w[:].bitcast(I32), in_=wb_words[0].bitcast(I32))
-        load_scale_rows((sy, sy, sy, sy), sx_s, sx_scales)
-        load_scale_rows((sy, sy, sy, sy), ws_s, ws_scales)
-        load_scale_rows((sy, sy, sy, sy), wb_s, wb_scales)
+        nc.sync.dma_start(out=sx_w[:].bitcast(I32), in_=words_view(sx_words))
+        nc.sync.dma_start(out=ws_w[:].bitcast(I32), in_=words_view(ws_words))
+        nc.sync.dma_start(out=wb_w[:].bitcast(I32), in_=wb_words[0].bitcast(I32))
+        load_scale_rows(nc.sync, sx_s, sx_scales)
+        load_scale_rows(nc.sync, ws_s, ws_scales)
+        load_scale_rows(nc.sync, wb_s, wb_scales)
 
         def first_stage(bank, t, words, scales):
             nc.tensor.matmul_mx(
@@ -114,11 +120,11 @@ def tile_list_oneforboth_shared_skip_scattered_kernel(
                 rhs=words, rhs_scale=scales, start=True, stop=True,
             )
 
-        def scatter_s(window, offsets, values):
-            nc.scalar.activation(window[:].indirect(offsets[:]), values, COPY)
+        def scatter_on_scalar(window, offsets, values):
+            nc.scalar.activation(window[:].indirect(offsets), values, COPY)
 
-        def scatter_v(window, offsets, values):
-            nc.vector.tensor_copy(window[:].indirect(offsets[:]), values)
+        def scatter_on_vector(window, offsets, values):
+            nc.vector.tensor_copy(window[:].indirect(offsets), values)
 
         a_sb = [keep.tile([P, J], F32, name=f"a_sb{t}") for t in range(PACK)]
         b_sb = [keep.tile([P, 2, J], F32, name=f"b_sb{u}") for u in range(2)]
@@ -126,9 +132,9 @@ def tile_list_oneforboth_shared_skip_scattered_kernel(
             a_ps = psum.tile([P, J], F32, name=f"a_ps{t}")
             first_stage(a_ps[:], t, xt_gw[:].bitcast(E2M1), xt_gs[:])
             nc.scalar.copy(a_sb[t][:], a_ps[:])
-        scatter_s(pw[0], a_list, a_sb[0][:])
-        scatter_v(pw[1], a_list, a_sb[1][:])
-        scatter_v(pw[3], a_list, a_sb[3][:])
+        scatter_on_scalar(pw[0], a_list[:], a_sb[0][:])
+        scatter_on_vector(pw[1], a_list[:], a_sb[1][:])
+        scatter_on_vector(pw[3], a_list[:], a_sb[3][:])
         for u in range(2):
             b_ps = psum.tile([P, 2, J], F32, name=f"b_ps{u}")
             for v in range(2):
@@ -137,12 +143,12 @@ def tile_list_oneforboth_shared_skip_scattered_kernel(
         a_ps = psum.tile([P, J], F32, name="a_ps2", tag="b_ps0")
         first_stage(a_ps[:], 2, xt_gw[:].bitcast(E2M1), xt_gs[:])
         nc.scalar.copy(a_sb[2][:], a_ps[:])
-        half = O // 2
-        halves = [slice(0, half), slice(half, O)]
-        list_halves = [slice(0, half // 16), slice(half // 16, O // 16)]
+
+        halves = [slice(0, HALF), slice(HALF, O)]
+        list_halves = [slice(0, HALF // GROUP), slice(HALF // GROUP, O // GROUP)]
         sums = [
-            (0, halves[0], psum.tile([P, half], F32, name="p0_lo", tag="b_ps1")),
-            (0, halves[1], psum.tile([P, half], F32, name="p0_hi", tag="a_ps3")),
+            (0, halves[0], psum.tile([P, HALF], F32, name="p0_lo", tag="b_ps1")),
+            (0, halves[1], psum.tile([P, HALF], F32, name="p0_hi", tag="a_ps3")),
             (1, slice(0, O), psum.tile([P, O], F32, name="p1", tag="b_ps0")),
         ]
         for h, cols, bank in sums:
@@ -150,59 +156,63 @@ def tile_list_oneforboth_shared_skip_scattered_kernel(
                 out=bank[:], lhsT=ws_w[:, h * P : (h + 1) * P].bitcast(E4M3), lhsT_scale=ws_s[:, h * P : (h + 1) * P],
                 rhs=sx_w[:, cols].bitcast(E4M3), rhs_scale=sx_s[:, cols], start=True, stop=False,
             )
-        scatter_v(pv[0], b_list, b_sb[0][:, 0, :])
-        scatter_s(pv[1], b_list, b_sb[0][:, 1, :])
-        scatter_s(pw[2], a_list, a_sb[2][:])
-        scatter_v(pv[2], b_list, b_sb[1][:, 0, :])
-        scatter_s(pv[3], b_list, b_sb[1][:, 1, :])
+        scatter_on_vector(pv[0], b_list[:], b_sb[0][:, 0, :])
+        scatter_on_scalar(pv[1], b_list[:], b_sb[0][:, 1, :])
+        scatter_on_scalar(pw[2], a_list[:], a_sb[2][:])
+        scatter_on_vector(pv[2], b_list[:], b_sb[1][:, 0, :])
+        scatter_on_scalar(pv[3], b_list[:], b_sb[1][:, 1, :])
 
         pg = [keep.tile([P, C], F32, name=f"pg{t}") for t in range(PACK)]
-        hid = [tail.tile([P, half, PACK], BF16, name=f"hid{u}", align_bytes=64, offset=3072 + 1024 * u) for u in range(2)]
-        rows = [keep.tile([P, PACK, half], BF16, name=f"rows{u}", align_bytes=64) for u in range(2)]
+        hid = [
+            tail.tile([P, HALF, PACK], BF16, name=f"hid{u}", align_bytes=64, offset=PAGE_BYTES + (u - 1) * HID_BYTES)
+            for u in range(2)
+        ]
+        rows = [keep.tile([P, PACK, HALF], BF16, name=f"rows{u}", align_bytes=64) for u in range(2)]
         hid_w = keep.tile([P, O], U32, name="hid_w", align_bytes=64)
         hid_s = keep.tile([P, O], U8, name="hid_s", align_bytes=64)
 
-        def read_s(t, u):
+        def read_on_scalar(t, u):
             nc.scalar.activation(rows[u][:, t, :], pg[t][:].indirect(read_list[:, list_halves[u]]), COPY)
 
-        def read_v(t, u):
+        def read_on_vector(t, u):
             nc.vector.tensor_copy(rows[u][:, t, :], pg[t][:].indirect(read_list[:, list_halves[u]]))
 
         def interleave(u):
-            nc.vector.tensor_copy(hid[u][:].rearrange("p (c i) t -> p c t i", i=4), rows[u][:].rearrange("p t (c i) -> p c t i", i=4))
+            nc.vector.tensor_copy(
+                hid[u][:].rearrange("p (c i) t -> p c t i", i=4), rows[u][:].rearrange("p t (c i) -> p c t i", i=4)
+            )
 
         def quantise(u):
             nc.vector.quantize_mx(
                 out=hid_w[:, halves[u]].bitcast(E5M2), scales=hid_s[:, halves[u]], in_=hid[u][:].rearrange("p o t -> p (o t)")
             )
 
-        def second_stage(h, cols, bank):
+        for t in range(PACK):
+            nc.vector.tensor_tensor(pg[t][:], pw[t][:], pv[t][:], ADD)
+        for t, u in ((0, 0), (1, 0), (3, 0), (0, 1), (3, 1)):
+            read_on_scalar(t, u)
+        read_on_vector(2, 0)
+        read_on_vector(2, 1)
+        interleave(0)
+        read_on_vector(1, 1)
+        quantise(0)
+        interleave(1)
+        page = [tail.tile([P, E], F32, name=f"page{h}", align_bytes=64, offset=PAGE_BYTES * h) for h in range(2)]
+        nc.vector.memset(page[0][:].bitcast(I32), 0)
+        quantise(1)
+        nc.vector.memset(page[1][:].bitcast(I32), 0)
+
+        p_sb = [keep.tile([P, O], F32, name=f"p_sb{h}") for h in range(2)]
+        for h, cols, bank in sums:
             nc.tensor.matmul_mx(
                 out=bank[:], lhsT=wb_w[:, 2 * h * P : 2 * (h + 1) * P].bitcast(E2M1), lhsT_scale=wb_s[:, h * P : (h + 1) * P],
                 rhs=hid_w[:, cols].bitcast(E5M2), rhs_scale=hid_s[:, cols], start=False, stop=True,
             )
-
-        for t in range(PACK):
-            nc.vector.tensor_tensor(pg[t][:], pw[t][:], pv[t][:], ADD)
-        for t, u in ((0, 0), (1, 0), (3, 0), (0, 1), (3, 1)):
-            read_s(t, u)
-        read_v(2, 0)
-        read_v(2, 1)
-        interleave(0)
-        read_v(1, 1)
-        quantise(0)
-        interleave(1)
-        page = [tail.tile([P, E], F32, name=f"page{h}", align_bytes=64, offset=4096 * h) for h in range(2)]
-        nc.vector.memset(page[0][:].bitcast(I32), 0)
-        quantise(1)
-        nc.vector.memset(page[1][:].bitcast(I32), 0)
-        p_sb = [keep.tile([P, O], F32, name=f"p_sb{h}") for h in range(2)]
-        for h, cols, bank in sums:
-            second_stage(h, cols, bank)
-        for u in range(2):
-            nc.scalar.copy(p_sb[0][:, halves[u]], sums[u][2][:])
-            nc.scalar.activation(page[0][:].indirect(page_list[:, list_halves[u]]), p_sb[0][:, halves[u]], COPY)
-        nc.vector.tensor_copy(p_sb[1][:], sums[2][2][:])
-        nc.vector.tensor_copy(page[1][:].indirect(page_list[:]), p_sb[1][:])
+        for (h, cols, bank), entries in zip(sums[:2], list_halves):
+            nc.scalar.copy(p_sb[h][:, cols], bank[:])
+            scatter_on_scalar(page[h], page_list[:, entries], p_sb[h][:, cols])
+        h, cols, bank = sums[2]
+        nc.vector.tensor_copy(p_sb[h][:], bank[:])
+        scatter_on_vector(page[h], page_list[:], p_sb[h][:])
         for h in range(2):
             nc.sync.dma_start(out=out[h * P : (h + 1) * P, :], in_=page[h][:])

from contextlib import ExitStack

import concourse.mybir as mybir

K, T, Z, J, R, C, O, N, L, E = 512, 1024, 1024, 256, 512, 512, 256, 256, 512, 1024
FLOPS = 2 * (2 * K * R * J + R * N * O + L * N * O)

F32 = mybir.dt.float32
BF16 = mybir.dt.bfloat16
I32 = mybir.dt.int32
U32 = mybir.dt.uint32
U16 = mybir.dt.uint16
U8 = mybir.dt.uint8
E4M3 = mybir.dt.float8_e4m3fn_x4
E5M2 = mybir.dt.float8_e5m2_x4
E2M1 = mybir.dt.float4_e2m1fn_x4
COPY = mybir.ActivationFunctionType.Copy
ADD = mybir.AluOpType.add

P = 128
PACK = 4
GROUP = 16
HALF = O // 2
LINE = 16
PAGE_BYTES = 4 * E
HID_BYTES = 2 * PACK * HALF


def load_scale_rows(queue, tile, scales):
    for q in range(4):
        queue.dma_start(out=tile[32 * q : 32 * q + 4, :].bitcast(I32), in_=scales[0, 4 * q : 4 * q + 4, :].bitcast(I32))


def words_view(words):
    return words[0].rearrange("p n t -> p (n t)").bitcast(I32)


def tile_list_oneforboth_shared_skip_scattered_kernel(
    tc, xt_words, xt_scales, xo_words, xo_scales, w_words, w_scales, wb_words, wb_scales,
    sx_words, sx_scales, ws_words, ws_scales, offs, offs2, offs3, offs4, offs5, offs6, out,
):
    nc = tc.nc
    with ExitStack() as ctx:
        lists = ctx.enter_context(tc.tile_pool(name="lists", bufs=1))
        keep = ctx.enter_context(tc.tile_pool(name="keep", bufs=1))
        tail = ctx.enter_context(tc.tile_pool(name="tail", bufs=1))
        psum = ctx.enter_context(tc.psum_pool(name="psum", bufs=1))

        tok_list = lists.tile([P, J // GROUP], U16, name="tok_list")
        note_list = lists.tile([P, J // GROUP], U16, name="note_list")
        a_list = lists.tile([P, J // GROUP], U16, name="a_list")
        b_list = lists.tile([P, J // GROUP], U16, name="b_list")
        read_list = lists.tile([P, O // GROUP], U16, name="read_list")
        page_list = lists.tile([P, O // GROUP], U16, name="page_list")

        xt_w = keep.tile([P, T], U16, name="xt_w", tag="late0", align_bytes=64)
        xo_w = keep.tile([P, Z], U32, name="xo_w", align_bytes=64)
        xt_s = keep.tile([P, T], U8, name="xt_s", tag="late2", align_bytes=64)
        xo_s = keep.tile([P, Z], U8, name="xo_s", align_bytes=64)
        w_w = keep.tile([P, R], U32, name="w_w", tag="late1", align_bytes=64)
        w_s = keep.tile([P, R], U8, name="w_s", align_bytes=64)
        late_s = keep.tile([P, 3 * N], U8, name="late_s", align_bytes=64)
        wb_s, sx_s, ws_s = late_s[:, 0:N], late_s[:, N : 2 * N], late_s[:, 2 * N : 3 * N]

        nc.vector.memset(xt_s[:].bitcast(I32), 0)
        nc.vector.memset(w_s[:].bitcast(I32), 0)
        nc.vector.memset(xo_s[:].bitcast(I32), 0)
        pw = [keep.tile([P, C], F32, name=f"pw{t}") for t in range(PACK)]
        pv = [keep.tile([P, C], F32, name=f"pv{t}") for t in range(PACK)]
        for board in pw + pv:
            nc.vector.memset(board[:].bitcast(I32), 0)
        nc.vector.memset(late_s[:].bitcast(I32), 0)

        nc.sync.dma_start(tok_list[:], offs)
        nc.sync.dma_start(out=xt_w[:].bitcast(I32), in_=xt_words[0].bitcast(I32))
        nc.sync.dma_start(out=w_w[:].bitcast(I32), in_=words_view(w_words))
        load_scale_rows(nc.scalar, xt_s, xt_scales)
        nc.sync.dma_start(out=xo_w[:].bitcast(I32), in_=words_view(xo_words))
        load_scale_rows(nc.sync, w_s, w_scales)
        nc.sync.dma_start(note_list[:], offs2)
        load_scale_rows(nc.sync, xo_s, xo_scales)
        nc.sync.dma_start(a_list[:], offs3)
        nc.sync.dma_start(b_list[:], offs4)
        nc.sync.dma_start(read_list[:], offs5)
        nc.sync.dma_start(page_list[:], offs6)

        xt_gw = keep.tile([P, J], U16, name="xt_gw", align_bytes=64)
        xt_gs = keep.tile([P, J], U8, name="xt_gs", align_bytes=64)
        xo_gw = keep.tile([P, J], U32, name="xo_gw", align_bytes=64)
        xo_gs = keep.tile([P, J], U8, name="xo_gs", align_bytes=64)
        wd_w = keep.tile([P, PACK, P], U32, name="wd_w", align_bytes=64)
        wd_s = keep.tile([P, PACK, P], U8, name="wd_s", align_bytes=64)

        nc.vector.tensor_copy(xt_gw[:], xt_w[:].indirect(tok_list[:]))
        nc.vector.tensor_copy(xt_gs[:], xt_s[:].indirect(tok_list[:]))
        nc.vector.tensor_copy(
            wd_w[:].rearrange("p t (c i) -> p c t i", i=LINE // 4),
            w_w[:].rearrange("p (c i t) -> p c t i", i=LINE // 4, t=PACK),
        )
        nc.vector.tensor_copy(
            wd_s[:].rearrange("p t (c i) -> p c t i", i=LINE),
            w_s[:].rearrange("p (c i t) -> p c t i", i=LINE, t=PACK),
        )
        nc.vector.tensor_copy(xo_gw[:], xo_w[:].indirect(note_list[:]))
        nc.vector.tensor_copy(xo_gs[:], xo_s[:].indirect(note_list[:]))

        sx_w = keep.tile([P, O], U32, name="sx_w", tag="late0", align_bytes=64)
        ws_w = keep.tile([P, N], U32, name="ws_w", tag="late1", align_bytes=64)
        wb_w = keep.tile([P, 2 * N], U8, name="wb_w", tag="late2", align_bytes=64)
        nc.sync.dma_start(out=sx_w[:].bitcast(I32), in_=words_view(sx_words))
        nc.sync.dma_start(out=ws_w[:].bitcast(I32), in_=words_view(ws_words))
        nc.sync.dma_start(out=wb_w[:].bitcast(I32), in_=wb_words[0].bitcast(I32))
        load_scale_rows(nc.sync, sx_s, sx_scales)
        load_scale_rows(nc.sync, ws_s, ws_scales)
        load_scale_rows(nc.sync, wb_s, wb_scales)

        def first_stage(bank, t, words, scales):
            nc.tensor.matmul_mx(
                out=bank, lhsT=wd_w[:, t, :].bitcast(E4M3), lhsT_scale=wd_s[:, t, :],
                rhs=words, rhs_scale=scales, start=True, stop=True,
            )

        def scatter_on_scalar(window, offsets, values):
            nc.scalar.activation(window[:].indirect(offsets), values, COPY)

        def scatter_on_vector(window, offsets, values):
            nc.vector.tensor_copy(window[:].indirect(offsets), values)

        a_sb = [keep.tile([P, J], F32, name=f"a_sb{t}") for t in range(PACK)]
        b_sb = [keep.tile([P, 2, J], F32, name=f"b_sb{u}") for u in range(2)]
        for t in (0, 1, 3):
            a_ps = psum.tile([P, J], F32, name=f"a_ps{t}")
            first_stage(a_ps[:], t, xt_gw[:].bitcast(E2M1), xt_gs[:])
            nc.scalar.copy(a_sb[t][:], a_ps[:])
        scatter_on_scalar(pw[0], a_list[:], a_sb[0][:])
        scatter_on_vector(pw[1], a_list[:], a_sb[1][:])
        scatter_on_vector(pw[3], a_list[:], a_sb[3][:])
        for u in range(2):
            b_ps = psum.tile([P, 2, J], F32, name=f"b_ps{u}")
            for v in range(2):
                first_stage(b_ps[:, v, :], 2 * u + v, xo_gw[:].bitcast(E4M3), xo_gs[:])
            nc.scalar.copy(b_sb[u][:], b_ps[:])
        a_ps = psum.tile([P, J], F32, name="a_ps2", tag="b_ps0")
        first_stage(a_ps[:], 2, xt_gw[:].bitcast(E2M1), xt_gs[:])
        nc.scalar.copy(a_sb[2][:], a_ps[:])

        halves = [slice(0, HALF), slice(HALF, O)]
        list_halves = [slice(0, HALF // GROUP), slice(HALF // GROUP, O // GROUP)]
        sums = [
            (0, halves[0], psum.tile([P, HALF], F32, name="p0_lo", tag="b_ps1")),
            (0, halves[1], psum.tile([P, HALF], F32, name="p0_hi", tag="a_ps3")),
            (1, slice(0, O), psum.tile([P, O], F32, name="p1", tag="b_ps0")),
        ]
        for h, cols, bank in sums:
            nc.tensor.matmul_mx(
                out=bank[:], lhsT=ws_w[:, h * P : (h + 1) * P].bitcast(E4M3), lhsT_scale=ws_s[:, h * P : (h + 1) * P],
                rhs=sx_w[:, cols].bitcast(E4M3), rhs_scale=sx_s[:, cols], start=True, stop=False,
            )
        scatter_on_vector(pv[0], b_list[:], b_sb[0][:, 0, :])
        scatter_on_scalar(pv[1], b_list[:], b_sb[0][:, 1, :])
        scatter_on_scalar(pw[2], a_list[:], a_sb[2][:])
        scatter_on_vector(pv[2], b_list[:], b_sb[1][:, 0, :])
        scatter_on_scalar(pv[3], b_list[:], b_sb[1][:, 1, :])

        pg = [keep.tile([P, C], F32, name=f"pg{t}") for t in range(PACK)]
        hid = [
            tail.tile([P, HALF, PACK], BF16, name=f"hid{u}", align_bytes=64, offset=PAGE_BYTES + (u - 1) * HID_BYTES)
            for u in range(2)
        ]
        rows = [keep.tile([P, PACK, HALF], BF16, name=f"rows{u}", align_bytes=64) for u in range(2)]
        hid_w = keep.tile([P, O], U32, name="hid_w", align_bytes=64)
        hid_s = keep.tile([P, O], U8, name="hid_s", align_bytes=64)

        def read_on_scalar(t, u):
            nc.scalar.activation(rows[u][:, t, :], pg[t][:].indirect(read_list[:, list_halves[u]]), COPY)

        def read_on_vector(t, u):
            nc.vector.tensor_copy(rows[u][:, t, :], pg[t][:].indirect(read_list[:, list_halves[u]]))

        def interleave(u):
            nc.vector.tensor_copy(
                hid[u][:].rearrange("p (c i) t -> p c t i", i=4), rows[u][:].rearrange("p t (c i) -> p c t i", i=4)
            )

        def quantise(u):
            nc.vector.quantize_mx(
                out=hid_w[:, halves[u]].bitcast(E5M2), scales=hid_s[:, halves[u]], in_=hid[u][:].rearrange("p o t -> p (o t)")
            )

        for t in range(PACK):
            nc.vector.tensor_tensor(pg[t][:], pw[t][:], pv[t][:], ADD)
        for t, u in ((0, 0), (1, 0), (3, 0), (0, 1), (3, 1)):
            read_on_scalar(t, u)
        read_on_vector(2, 0)
        read_on_vector(2, 1)
        interleave(0)
        read_on_vector(1, 1)
        quantise(0)
        interleave(1)
        page = [tail.tile([P, E], F32, name=f"page{h}", align_bytes=64, offset=PAGE_BYTES * h) for h in range(2)]
        nc.vector.memset(page[0][:].bitcast(I32), 0)
        quantise(1)
        nc.vector.memset(page[1][:].bitcast(I32), 0)

        p_sb = [keep.tile([P, O], F32, name=f"p_sb{h}") for h in range(2)]
        for h, cols, bank in sums:
            nc.tensor.matmul_mx(
                out=bank[:], lhsT=wb_w[:, 2 * h * P : 2 * (h + 1) * P].bitcast(E2M1), lhsT_scale=wb_s[:, h * P : (h + 1) * P],
                rhs=hid_w[:, cols].bitcast(E5M2), rhs_scale=hid_s[:, cols], start=False, stop=True,
            )
        for (h, cols, bank), entries in zip(sums[:2], list_halves):
            nc.scalar.copy(p_sb[h][:, cols], bank[:])
            scatter_on_scalar(page[h], page_list[:, entries], p_sb[h][:, cols])
        h, cols, bank = sums[2]
        nc.vector.tensor_copy(p_sb[h][:], bank[:])
        scatter_on_vector(page[h], page_list[:], p_sb[h][:])
        for h in range(2):
            nc.sync.dma_start(out=out[h * P : (h + 1) * P, :], in_=page[h][:])
